import numpy as np, ml_dtypes
CORES = [3,5,43,45,51,53,67,69,75,77,83,85,91,93,115,117]
N = 16
import mx_ref
NC = 512
SEQ = [0,0,1,1,1,1,2,2,2,3,3,3,3,4,4,4]
WID = [128,220,388,292,510,320,144,484,326,358,402,304,256,426,146,512]
BF = ml_dtypes.bfloat16
def setup_inputs(rng):
    def f(*shape):
        return mx_ref.flush((rng.standard_normal(shape, dtype=np.float32) * np.exp2(rng.integers(-2, 3, shape[:-1] + (1,)))).astype(BF))
    return {"w": f(N, 128, 512), "x": f(N, 128, 4 * NC)}
def setup_inputs_blocks(rng):
    d = setup_inputs(rng)
    for k in ("w", "x"): d[k] = mx_ref.spread(d[k], rng, 4)
    return d
def setup_inputs_wide(rng):
    d = setup_inputs(rng)
    for k in ("w", "x"): d[k] = mx_ref.flush((d[k].astype(np.float32) * np.exp2(rng.integers(-10, 11, (N, 1, 1))).astype(np.float32)).astype(BF))
    return d
def reference(w, x):
    y = np.full((N, 128, 1510), np.nan, np.float32)
    for r in range(N):
        qw = mx_ref.quantize(w[r]); a = 0
        for j in range(N):
            if SEQ[j] == SEQ[r]:
                y[r][:, a:a + WID[j]] = mx_ref.matmul(qw, mx_ref.quantize(x[j][:, :4 * WID[j]])); a += WID[j]
    return {"y": y}

@@ -1,0 +1,190 @@
+from concourse.bass import DstId, RemoteDMATransfer
+from concourse.mybir import dt, ActivationFunctionType
+
+SLOT = 512
+FIRST = 128
+
+SCRATCH = {
+    "xb": ("sbuf", [128, 4 * SLOT], "bfloat16"),
+    "wb": ("sbuf", [128, 512], "bfloat16"),
+    "xq": ("sbuf", [128, 4 * SLOT], "float8_e4m3fn_x4"),
+    "xs": ("sbuf", [128, 4 * SLOT], "uint8"),
+    "wq": ("sbuf", [128, 128], "float8_e4m3fn_x4"),
+    "ws": ("sbuf", [128, 128], "uint8"),
+    "ysb": ("sbuf", [128, 1510], "float32"),
+    "ps": ("psum", [128, 512 * 8], "float32"),
+}
+SEMAPHORES = (["ldx0", "ldx1", "ldw", "qx0", "qx1", "qw", "st", "sc", "sp", "sf"]
+              + ["a%s%d%d" % (p, k, h) for p in "pc" for k in range(4) for h in range(2)]
+              + ["mm%d" % b for b in range(8)] + ["cp%d" % b for b in range(8)])
+
+_CACHE = {}
+
+
+def _bits(m):
+    return [b for b in range(m.bit_length()) if (m >> b) & 1]
+
+
+def _plan(T, topo):
+    if "plan" in _CACHE:
+        return _CACHE["plan"]
+    cores, SEQ, WID = list(T.cores), T.tables["SEQ"], T.tables["WID"]
+    n, ncores, group = len(cores), topo.CHIPS * topo.CORES_PER_CHIP, set(T.cores)
+    chip, die, may = topo.chip, topo.die, topo.may_write
+    slot, yoff, pieces = {}, {}, {}
+    for j in range(n):
+        before = [i for i in range(j) if SEQ[i] == SEQ[j]]
+        slot[j], yoff[j] = len(before), sum(WID[i] for i in before)
+        pieces[j] = [(0, FIRST), (FIRST, WID[j])] if WID[j] >= 2 * FIRST else [(0, WID[j])]
+    ops, need, arr, key = {}, {}, {}, {}
+
+    def engines(c):
+        wide, narrow = 0, None
+        for o in range(ncores):
+            if o != c:
+                m = topo.mask(c, o)
+                wide |= m
+                narrow = m if narrow is None else narrow & m
+        return _bits(wide), _bits(narrow), _bits(wide & ~narrow)
+
+    def emit(prio, src, j, item, xfers, lsem, hops, late, relay):
+        ops.setdefault(src, []).append((prio, j, item, xfers, lsem))
+        part, h0, h1 = item
+        sem = "a%s%d%d" % (part, slot[j], h0)
+        for dsts, eng in xfers:
+            for d in dsts:
+                arr[(d, j, item)] = (sem, len(eng))
+                for h in range(h0, h1 + 1):
+                    need.setdefault((d, j, h), []).append((sem, len(eng)))
+                    key[(d, j, h)] = 2 * hops + (1.5 if late else h) + (0.1 if relay else 0.0)
+
+    for j in range(n):
+        src, last = cores[j], len(pieces[j]) - 1
+        e_all, e_off, e_hi = engines(src)
+        peers = [cores[i] for i in range(n) if SEQ[i] == SEQ[j] and i != j]
+        on = [p for p in peers if chip(p) == chip(src)]
+        entries, fwd, relay = [], {}, []
+        for ch in sorted(set(chip(p) for p in peers if chip(p) != chip(src))):
+            grp = [p for p in peers if chip(p) == ch]
+            if all(may(src, p) for p in grp):
+                e = ([p for p in grp if die(p) == die(src)] + grp)[0]
+                entries.append(e)
+                fwd[e] = [p for p in grp if p != e]
+            else:
+                relay += grp
+        whole = [("p", 0, last), ("c", 0, last)]
+        chunked = [("p", 0, 0), ("c", 0, 0), ("c", 1, 1), ("p", 1, 1)] if last else whole
+
+        def direct(prio, items, xfers, lsem, late):
+            for it in items:
+                emit(prio, src, j, it, xfers, lsem, 1, late, False)
+                for e in entries:
+                    if fwd[e] and any(e in dsts for dsts, _ in xfers):
+                        emit(2, e, j, it, [(fwd[e], engines(e)[0])], "sf", 2, late, False)
+
+        if relay:
+            helpers = [h for h in range(ncores) if chip(h) == chip(src) and die(h) == die(src)
+                       and h not in group and all(may(h, d) for d in relay)]
+            share = {}
+            for i, d in enumerate(relay):
+                share.setdefault(helpers[i % len(helpers)], []).append(d)
+            for it in chunked:
+                emit(0, src, j, it, [(sorted(share), e_all)], "sc", 1, False, False)
+                for h in sorted(share):
+                    emit(2, h, j, it, [(share[h], engines(h)[1])], "sf", 2, False, True)
+            xf = ([(entries, e_off)] if entries else []) + ([(on, e_hi if entries else e_all)] if on else [])
+            if xf:
+                direct(1, whole, xf, "sp", True)
+        elif entries:
+            direct(0, chunked, [(entries, e_off)], "sc", False)
+            if on:
+                direct(1, whole, [(on, e_hi)], "sp", True)
+        else:
+            direct(0, chunked, [(on, e_all)], "sc", False)
+    _CACHE["plan"] = (slot, yoff, pieces, ops, need, arr, key)
+    return _CACHE["plan"]
+
+
+def rank_program(g, core, T, topo):
+    slot, yoff, pieces, ops, need, arr, key = _plan(T, topo)
+    cores, SEQ = list(T.cores), T.tables["SEQ"]
+    rank = T.rank_of(core)
+    mine = sorted(ops.get(core, []), key=lambda o: o[0])
+    if rank is None and not mine:
+        return
+    totals = {}
+    for _, _, _, xfers, lsem in mine:
+        totals[lsem] = totals.get(lsem, 0) + sum(len(eng) for _, eng in xfers)
+
+    def view(j, part, c0, c1):
+        a = SLOT * slot[j]
+        if part == "p":
+            return T.xs[:, a + c0:a + c1]
+        return T.xq[:, a + c0:a + c1].bitcast(dt.uint8)
+
+    if rank is not None:
+        a = SLOT * slot[rank]
+        for h, (c0, c1) in enumerate(pieces[rank]):
+            g.sync.dma_start(T.xb[:, 4 * c0:4 * c1], T.x[:, 4 * c0:4 * c1]).then_inc(T.sem["ldx%d" % h], 16)
+        g.sync.dma_start(T.wb[:], T.w[:]).then_inc(T.sem.ldw, 16)
+        for h, (c0, c1) in enumerate(pieces[rank]):
+            g.vector.wait_ge(T.sem["ldx%d" % h], 16)
+            g.vector.quantize_mx(T.xq[:, a + c0:a + c1], T.xs[:, a + c0:a + c1],
+                                 T.xb[:, 4 * c0:4 * c1]).then_inc(T.sem["qx%d" % h], 1)
+        g.vector.wait_ge(T.sem.ldw, 16)
+        g.vector.quantize_mx(T.wq[:], T.ws[:], T.wb[:]).then_inc(T.sem.qw, 1)
+
+    seen = {}
+
+    def wait(q, tag, sem, val):
+        if seen.get((tag, sem), 0) < val:
+            q.wait_ge(T.sem[sem], val)
+            seen[(tag, sem)] = val
+
+    for _, j, item, xfers, lsem in mine:
+        part, h0, h1 = item
+        if cores[j] == core:
+            for h in range(h0, h1 + 1):
+                wait(g, "g", "qx%d" % h, 1)
+        else:
+            wait(g, "g", *arr[(core, j, item)])
+        ap = view(j, part, pieces[j][h0][0], pieces[j][h1][1])
+        sem = T.sem["a%s%d%d" % (part, slot[j], h0)]
+        trs = []
+        for dsts, eng in xfers:
+            ids = []
+            for d in dsts:
+                rid, pid, _ = topo.addr(d)
+                ids.append(DstId(rid=rid, pnc=pid))
+            trs.append(RemoteDMATransfer(dst_ids=ids, dma_engine_mask=sum(1 << b for b in eng), remote_sem=sem,
+                                         srcs=[ap], dsts=[ap for _ in dsts]))
+        g.remote_dma_fused(trs, local_sem=T.sem[lsem])
+    for lsem in sorted(totals):
+        g.wait_ge(T.sem[lsem], totals[lsem])
+    if rank is None:
+        return
+
+    blocks = sorted((0.0 if j == rank else key[(core, j, h)], j, h)
+                    for j in range(len(cores)) if SEQ[j] == SEQ[rank] for h in range(len(pieces[j])))
+    g.tensor.wait_ge(T.sem.qw, 1)
+    g.sync.wait_ge(T.sem.sc, totals["sc"])
+    for b, (_, j, h) in enumerate(blocks):
+        if j == rank:
+            wait(g.tensor, "t", "qx%d" % h, 1)
+        else:
+            for sem, val in need[(core, j, h)]:
+                wait(g.tensor, "t", sem, val)
+        c0, c1 = pieces[j][h]
+        a, y0, y1 = SLOT * slot[j], yoff[j] + c0, yoff[j] + c1
+        g.tensor.matmul_mx(T.ps[:, 512 * b:512 * b + c1 - c0], T.wq[:], T.ws[:], T.xq[:, a + c0:a + c1],
+                           T.xs[:, a + c0:a + c1], True, True).then_inc(T.sem["mm%d" % b], 1)
+        if b % 2 == 0:
+            g.vector.wait_ge(T.sem["mm%d" % b], 1)
+            g.vector.tensor_copy(T.ysb[:, y0:y1], T.ps[:, 512 * b:512 * b + c1 - c0]).then_inc(T.sem["cp%d" % b], 1)
+        else:
+            g.scalar.wait_ge(T.sem["mm%d" % b], 1)
+            g.scalar.activation(T.ysb[:, y0:y1], T.ps[:, 512 * b:512 * b + c1 - c0],
+                                ActivationFunctionType.Copy).then_inc(T.sem["cp%d" % b], 1)
+        g.sync.wait_ge(T.sem["cp%d" % b], 1)
+        g.sync.dma_start(T.y[:, y0:y1], T.ysb[:, y0:y1]).then_inc(T.sem.st, 16)
+    g.sync.wait_ge(T.sem.st, 16 * len(blocks))

@@ -29,7 +29,7 @@ def _plan(T, topo):
     if "plan" in _CACHE:
         return _CACHE["plan"]
     cores, SEQ, WID = list(T.cores), T.tables["SEQ"], T.tables["WID"]
-    n, ncores, group = len(cores), topo.CHIPS * topo.CORES_PER_CHIP, set(T.cores)
+    n, ncores, taken = len(cores), topo.CHIPS * topo.CORES_PER_CHIP, set(T.cores)
     chip, die, may = topo.chip, topo.die, topo.may_write
     slot, yoff, pieces = {}, {}, {}
     for j in range(n):
@@ -47,16 +47,17 @@ def _plan(T, topo):
                 narrow = m if narrow is None else narrow & m
         return _bits(wide), _bits(narrow), _bits(wide & ~narrow)
 
-    def emit(prio, src, j, item, xfers, lsem, hops, late, relay):
-        ops.setdefault(src, []).append((prio, j, item, xfers, lsem))
-        part, h0, h1 = item
+    def emit(prio, src, j, kind, xfers, lsem, hops, late, relay):
+        ops.setdefault(src, []).append((prio, j, kind, xfers, lsem))
+        part, h0, h1 = kind
         sem = "a%s%d%d" % (part, slot[j], h0)
-        for dsts, eng in xfers:
+        for dsts, eng, u, v in xfers:
             for d in dsts:
-                arr[(d, j, item)] = (sem, len(eng))
+                arr[(d, j, kind)] = (sem, len(eng))
+                key[(d, j)] = 2 * hops + (0.5 if late else 0.0) + (0.1 if relay else 0.0)
                 for h in range(h0, h1 + 1):
-                    need.setdefault((d, j, h), []).append((sem, len(eng)))
-                    key[(d, j, h)] = 2 * hops + (1.5 if late else h) + (0.1 if relay else 0.0)
+                    t = need.setdefault((d, j, h), {})
+                    t[sem] = t.get(sem, 0) + len(eng)
 
     for j in range(n):
         src, last = cores[j], len(pieces[j]) - 1
@@ -73,30 +74,63 @@ def _plan(T, topo):
             else:
                 relay += grp
         whole = [("p", 0, last), ("c", 0, last)]
-        chunked = [("p", 0, 0), ("c", 0, 0), ("c", 1, 1), ("p", 1, 1)] if last else whole
+        chunked = [("c", 0, 0), ("c", 1, 1), ("p", 0, 1)] if last else whole
+        idle = [h for h in range(ncores) if chip(h) == chip(src) and h not in taken
+                and all(may(h, d) for d in relay + entries)]
+        near = [h for h in idle if die(h) == die(src)]
+        far = [h for h in idle if die(h) != die(src)]
 
-        def direct(prio, items, xfers, lsem, late):
-            for it in items:
-                emit(prio, src, j, it, xfers, lsem, 1, late, False)
+        def span(kind):
+            return pieces[j][kind[1]][0], pieces[j][kind[2]][1]
+
+        def direct(prio, kinds, pairs, lsem, late):
+            for kd in kinds:
+                u, v = span(kd)
+                emit(prio, src, j, kd, [(dsts, eng, u, v) for dsts, eng in pairs], lsem, 1, late, False)
                 for e in entries:
-                    if fwd[e] and any(e in dsts for dsts, _ in xfers):
-                        emit(2, e, j, it, [(fwd[e], engines(e)[0])], "sf", 2, late, False)
+                    if fwd[e] and any(e in dsts for dsts, _ in pairs):
+                        emit(2, e, j, kd, [(fwd[e], engines(e)[0], u, v)], "sf", 2, late, False)
 
         if relay:
-            helpers = [h for h in range(ncores) if chip(h) == chip(src) and die(h) == die(src)
-                       and h not in group and all(may(h, d) for d in relay)]
-            share = {}
-            for i, d in enumerate(relay):
-                share.setdefault(helpers[i % len(helpers)], []).append(d)
-            for it in chunked:
-                emit(0, src, j, it, [(sorted(share), e_all)], "sc", 1, False, False)
-                for h in sorted(share):
-                    emit(2, h, j, it, [(share[h], engines(h)[1])], "sf", 2, False, True)
-            xf = ([(entries, e_off)] if entries else []) + ([(on, e_hi if entries else e_all)] if on else [])
-            if xf:
-                direct(1, whole, xf, "sp", True)
+            if len(relay) == 1 and near and far:
+                lanes = [(near[0], relay, 0, 1, 2), (far[0], relay, 1, 2, 2)]
+            elif len(relay) == 2 and len(near) >= 2 and far:
+                lanes = [(near[0], relay[:1], 0, 2, 3), (near[1], relay[1:], 0, 2, 3), (far[0], relay, 2, 3, 3)]
+            else:
+                lanes = [(idle[i % len(idle)], [d], 0, 1, 1) for i, d in enumerate(relay)]
+            for kd in chunked:
+                c0, c1 = span(kd)
+                ranges = {}
+                for h, dsts, a0, a1, den in lanes:
+                    taken.add(h)
+                    u, v = c0 + (c1 - c0) * a0 // den // 2 * 2, c0 + (c1 - c0) * a1 // den // 2 * 2
+                    ranges.setdefault((u, v), []).append((h, dsts))
+                widths = {}
+                for u, v in sorted(ranges):
+                    widths.setdefault(v - u, []).append((u, v))
+                for wd in sorted(widths, reverse=True):
+                    rs = widths[wd]
+                    k = len(e_all) // len(rs)
+                    emit(0, src, j, kd, [([h for h, _ in ranges[r]], e_all[i * k:(i + 1) * k], r[0], r[1])
+                                         for i, r in enumerate(rs)], "sc", 1, False, False)
+                    for r in rs:
+                        for h, dsts in ranges[r]:
+                            emit(2, h, j, kd, [(dsts, engines(h)[1], r[0], r[1])], "sf", 2, False, True)
+            pairs = ([(entries, e_off)] if entries else []) + ([(on, e_hi if entries else e_all)] if on else [])
+            if pairs:
+                direct(1, whole, pairs, "sp", True)
         elif entries:
-            direct(0, chunked, [(entries, e_off)], "sc", False)
+            if len(entries) == 2 and 2 * WID[j] > SLOT and near and not any(fwd[e] for e in entries):
+                taken.add(near[0])
+                for kd in chunked:
+                    c0, c1 = span(kd)
+                    x = c0 + (c1 - c0) // 3 // 2 * 2
+                    emit(0, src, j, kd, [(entries[1:], e_off, x, c1), (near[:1], e_hi, x, c1)],
+                         "sc", 1, False, False)
+                    emit(0, src, j, kd, [(entries, e_off, c0, x)], "sc", 1, False, False)
+                    emit(2, near[0], j, kd, [(entries[:1], engines(near[0])[1], x, c1)], "sf", 2, False, True)
+            else:
+                direct(0, chunked, [(entries, e_off)], "sc", False)
             if on:
                 direct(1, whole, [(on, e_hi)], "sp", True)
         else:
@@ -107,14 +141,14 @@ def _plan(T, topo):
 
 def rank_program(g, core, T, topo):
     slot, yoff, pieces, ops, need, arr, key = _plan(T, topo)
-    cores, SEQ = list(T.cores), T.tables["SEQ"]
+    cores, SEQ, WID = list(T.cores), T.tables["SEQ"], T.tables["WID"]
     rank = T.rank_of(core)
     mine = sorted(ops.get(core, []), key=lambda o: o[0])
     if rank is None and not mine:
         return
     totals = {}
     for _, _, _, xfers, lsem in mine:
-        totals[lsem] = totals.get(lsem, 0) + sum(len(eng) for _, eng in xfers)
+        totals[lsem] = totals.get(lsem, 0) + sum(len(x[1]) for x in xfers)
 
     def view(j, part, c0, c1):
         a = SLOT * slot[j]
@@ -141,18 +175,17 @@ def rank_program(g, core, T, topo):
             q.wait_ge(T.sem[sem], val)
             seen[(tag, sem)] = val
 
-    for _, j, item, xfers, lsem in mine:
-        part, h0, h1 = item
+    for _, j, kind, xfers, lsem in mine:
+        part, h0, h1 = kind
         if cores[j] == core:
             for h in range(h0, h1 + 1):
                 wait(g, "g", "qx%d" % h, 1)
         else:
-            wait(g, "g", *arr[(core, j, item)])
-        ap = view(j, part, pieces[j][h0][0], pieces[j][h1][1])
+            wait(g, "g", *arr[(core, j, kind)])
         sem = T.sem["a%s%d%d" % (part, slot[j], h0)]
         trs = []
-        for dsts, eng in xfers:
-            ids = []
+        for dsts, eng, u, v in xfers:
+            ap, ids = view(j, part, u, v), []
             for d in dsts:
                 rid, pid, _ = topo.addr(d)
                 ids.append(DstId(rid=rid, pnc=pid))
@@ -164,27 +197,35 @@ def rank_program(g, core, T, topo):
     if rank is None:
         return
 
-    blocks = sorted((0.0 if j == rank else key[(core, j, h)], j, h)
-                    for j in range(len(cores)) if SEQ[j] == SEQ[rank] for h in range(len(pieces[j])))
+    tiles = sorted((0.0 if j == rank else key[(core, j)], WID[j], j)
+                   for j in range(len(cores)) if SEQ[j] == SEQ[rank])
     g.tensor.wait_ge(T.sem.qw, 1)
     g.sync.wait_ge(T.sem.sc, totals["sc"])
-    for b, (_, j, h) in enumerate(blocks):
-        if j == rank:
-            wait(g.tensor, "t", "qx%d" % h, 1)
-        else:
-            for sem, val in need[(core, j, h)]:
-                wait(g.tensor, "t", sem, val)
-        c0, c1 = pieces[j][h]
-        a, y0, y1 = SLOT * slot[j], yoff[j] + c0, yoff[j] + c1
-        g.tensor.matmul_mx(T.ps[:, 512 * b:512 * b + c1 - c0], T.wq[:], T.ws[:], T.xq[:, a + c0:a + c1],
-                           T.xs[:, a + c0:a + c1], True, True).then_inc(T.sem["mm%d" % b], 1)
-        if b % 2 == 0:
-            g.vector.wait_ge(T.sem["mm%d" % b], 1)
-            g.vector.tensor_copy(T.ysb[:, y0:y1], T.ps[:, 512 * b:512 * b + c1 - c0]).then_inc(T.sem["cp%d" % b], 1)
-        else:
-            g.scalar.wait_ge(T.sem["mm%d" % b], 1)
-            g.scalar.activation(T.ysb[:, y0:y1], T.ps[:, 512 * b:512 * b + c1 - c0],
-                                ActivationFunctionType.Copy).then_inc(T.sem["cp%d" % b], 1)
-        g.sync.wait_ge(T.sem["cp%d" % b], 1)
-        g.sync.dma_start(T.y[:, y0:y1], T.ysb[:, y0:y1]).then_inc(T.sem.st, 16)
-    g.sync.wait_ge(T.sem.st, 16 * len(blocks))
+    b = 0
+    for _, _, j in tiles:
+        hs = list(range(len(pieces[j])))
+        if j != rank:
+            hs.reverse()
+        for h in hs:
+            if j == rank:
+                wait(g.tensor, "t", "qx%d" % h, 1)
+            else:
+                for sem in sorted(need[(core, j, h)]):
+                    wait(g.tensor, "t", sem, need[(core, j, h)][sem])
+            c0, c1 = pieces[j][h]
+            a, y0, y1 = SLOT * slot[j], yoff[j] + c0, yoff[j] + c1
+            g.tensor.matmul_mx(T.ps[:, 512 * b:512 * b + c1 - c0], T.wq[:], T.ws[:], T.xq[:, a + c0:a + c1],
+                               T.xs[:, a + c0:a + c1], True, True).then_inc(T.sem["mm%d" % b], 1)
+            if b % 2 == 0:
+                g.vector.wait_ge(T.sem["mm%d" % b], 1)
+                g.vector.tensor_copy(T.ysb[:, y0:y1],
+                                     T.ps[:, 512 * b:512 * b + c1 - c0]).then_inc(T.sem["cp%d" % b], 1)
+            else:
+                g.scalar.wait_ge(T.sem["mm%d" % b], 1)
+                g.scalar.activation(T.ysb[:, y0:y1], T.ps[:, 512 * b:512 * b + c1 - c0],
+                                    ActivationFunctionType.Copy).then_inc(T.sem["cp%d" % b], 1)
+            g.sync.wait_ge(T.sem["cp%d" % b], 1)
+            b += 1
+        g.sync.dma_start(T.y[:, yoff[j]:yoff[j] + WID[j]],
+                         T.ysb[:, yoff[j]:yoff[j] + WID[j]]).then_inc(T.sem.st, 16)
+    g.sync.wait_ge(T.sem.st, 16 * len(tiles))

from concourse.bass import DstId, RemoteDMATransfer
from concourse.mybir import dt, ActivationFunctionType

SLOT = 512
FIRST = 128

SCRATCH = {
    "xb": ("sbuf", [128, 4 * SLOT], "bfloat16"),
    "wb": ("sbuf", [128, 512], "bfloat16"),
    "xq": ("sbuf", [128, 4 * SLOT], "float8_e4m3fn_x4"),
    "xs": ("sbuf", [128, 4 * SLOT], "uint8"),
    "wq": ("sbuf", [128, 128], "float8_e4m3fn_x4"),
    "ws": ("sbuf", [128, 128], "uint8"),
    "ysb": ("sbuf", [128, 1510], "float32"),
    "ps": ("psum", [128, 512 * 8], "float32"),
}
SEMAPHORES = (["ldx0", "ldx1", "ldw", "qx0", "qx1", "qw", "st", "sc", "sp", "sf"]
              + ["a%s%d%d" % (p, k, h) for p in "pc" for k in range(4) for h in range(2)]
              + ["mm%d" % b for b in range(8)] + ["cp%d" % b for b in range(8)])

_CACHE = {}


def _bits(m):
    return [b for b in range(m.bit_length()) if (m >> b) & 1]


def _plan(T, topo):
    if "plan" in _CACHE:
        return _CACHE["plan"]
    cores, SEQ, WID = list(T.cores), T.tables["SEQ"], T.tables["WID"]
    n, ncores, taken = len(cores), topo.CHIPS * topo.CORES_PER_CHIP, set(T.cores)
    chip, die, may = topo.chip, topo.die, topo.may_write
    slot, yoff, pieces = {}, {}, {}
    for j in range(n):
        before = [i for i in range(j) if SEQ[i] == SEQ[j]]
        slot[j], yoff[j] = len(before), sum(WID[i] for i in before)
        pieces[j] = [(0, FIRST), (FIRST, WID[j])] if WID[j] >= 2 * FIRST else [(0, WID[j])]
    ops, need, arr, key = {}, {}, {}, {}

    def engines(c):
        wide, narrow = 0, None
        for o in range(ncores):
            if o != c:
                m = topo.mask(c, o)
                wide |= m
                narrow = m if narrow is None else narrow & m
        return _bits(wide), _bits(narrow), _bits(wide & ~narrow)

    def emit(prio, src, j, kind, xfers, lsem, hops, late, relay):
        ops.setdefault(src, []).append((prio, j, kind, xfers, lsem))
        part, h0, h1 = kind
        sem = "a%s%d%d" % (part, slot[j], h0)
        for dsts, eng, u, v in xfers:
            for d in dsts:
                arr[(d, j, kind)] = (sem, len(eng))
                key[(d, j)] = 2 * hops + (0.5 if late else 0.0) + (0.1 if relay else 0.0)
                for h in range(h0, h1 + 1):
                    t = need.setdefault((d, j, h), {})
                    t[sem] = t.get(sem, 0) + len(eng)

    for j in range(n):
        src, last = cores[j], len(pieces[j]) - 1
        e_all, e_off, e_hi = engines(src)
        peers = [cores[i] for i in range(n) if SEQ[i] == SEQ[j] and i != j]
        on = [p for p in peers if chip(p) == chip(src)]
        entries, fwd, relay = [], {}, []
        for ch in sorted(set(chip(p) for p in peers if chip(p) != chip(src))):
            grp = [p for p in peers if chip(p) == ch]
            if all(may(src, p) for p in grp):
                e = ([p for p in grp if die(p) == die(src)] + grp)[0]
                entries.append(e)
                fwd[e] = [p for p in grp if p != e]
            else:
                relay += grp
        whole = [("p", 0, last), ("c", 0, last)]
        chunked = [("c", 0, 0), ("c", 1, 1), ("p", 0, 1)] if last else whole
        idle = [h for h in range(ncores) if chip(h) == chip(src) and h not in taken
                and all(may(h, d) for d in relay + entries)]
        near = [h for h in idle if die(h) == die(src)]
        far = [h for h in idle if die(h) != die(src)]

        def span(kind):
            return pieces[j][kind[1]][0], pieces[j][kind[2]][1]

        def direct(prio, kinds, pairs, lsem, late):
            for kd in kinds:
                u, v = span(kd)
                emit(prio, src, j, kd, [(dsts, eng, u, v) for dsts, eng in pairs], lsem, 1, late, False)
                for e in entries:
                    if fwd[e] and any(e in dsts for dsts, _ in pairs):
                        emit(2, e, j, kd, [(fwd[e], engines(e)[0], u, v)], "sf", 2, late, False)

        if relay:
            if len(relay) == 1 and near and far:
                lanes = [(near[0], relay, 0, 1, 2), (far[0], relay, 1, 2, 2)]
            elif len(relay) == 2 and len(near) >= 2 and far:
                lanes = [(near[0], relay[:1], 0, 2, 3), (near[1], relay[1:], 0, 2, 3), (far[0], relay, 2, 3, 3)]
            else:
                lanes = [(idle[i % len(idle)], [d], 0, 1, 1) for i, d in enumerate(relay)]
            for kd in chunked:
                c0, c1 = span(kd)
                ranges = {}
                for h, dsts, a0, a1, den in lanes:
                    taken.add(h)
                    u, v = c0 + (c1 - c0) * a0 // den // 2 * 2, c0 + (c1 - c0) * a1 // den // 2 * 2
                    ranges.setdefault((u, v), []).append((h, dsts))
                widths = {}
                for u, v in sorted(ranges):
                    widths.setdefault(v - u, []).append((u, v))
                for wd in sorted(widths, reverse=True):
                    rs = widths[wd]
                    k = len(e_all) // len(rs)
                    emit(0, src, j, kd, [([h for h, _ in ranges[r]], e_all[i * k:(i + 1) * k], r[0], r[1])
                                         for i, r in enumerate(rs)], "sc", 1, False, False)
                    for r in rs:
                        for h, dsts in ranges[r]:
                            emit(2, h, j, kd, [(dsts, engines(h)[1], r[0], r[1])], "sf", 2, False, True)
            pairs = ([(entries, e_off)] if entries else []) + ([(on, e_hi if entries else e_all)] if on else [])
            if pairs:
                direct(1, whole, pairs, "sp", True)
        elif entries:
            if len(entries) == 2 and 2 * WID[j] > SLOT and near and not any(fwd[e] for e in entries):
                taken.add(near[0])
                for kd in chunked:
                    c0, c1 = span(kd)
                    x = c0 + (c1 - c0) // 3 // 2 * 2
                    emit(0, src, j, kd, [(entries[1:], e_off, x, c1), (near[:1], e_hi, x, c1)],
                         "sc", 1, False, False)
                    emit(0, src, j, kd, [(entries, e_off, c0, x)], "sc", 1, False, False)
                    emit(2, near[0], j, kd, [(entries[:1], engines(near[0])[1], x, c1)], "sf", 2, False, True)
            else:
                direct(0, chunked, [(entries, e_off)], "sc", False)
            if on:
                direct(1, whole, [(on, e_hi)], "sp", True)
        else:
            direct(0, chunked, [(on, e_all)], "sc", False)
    _CACHE["plan"] = (slot, yoff, pieces, ops, need, arr, key)
    return _CACHE["plan"]


def rank_program(g, core, T, topo):
    slot, yoff, pieces, ops, need, arr, key = _plan(T, topo)
    cores, SEQ, WID = list(T.cores), T.tables["SEQ"], T.tables["WID"]
    rank = T.rank_of(core)
    mine = sorted(ops.get(core, []), key=lambda o: o[0])
    if rank is None and not mine:
        return
    totals = {}
    for _, _, _, xfers, lsem in mine:
        totals[lsem] = totals.get(lsem, 0) + sum(len(x[1]) for x in xfers)

    def view(j, part, c0, c1):
        a = SLOT * slot[j]
        if part == "p":
            return T.xs[:, a + c0:a + c1]
        return T.xq[:, a + c0:a + c1].bitcast(dt.uint8)

    if rank is not None:
        a = SLOT * slot[rank]
        for h, (c0, c1) in enumerate(pieces[rank]):
            g.sync.dma_start(T.xb[:, 4 * c0:4 * c1], T.x[:, 4 * c0:4 * c1]).then_inc(T.sem["ldx%d" % h], 16)
        g.sync.dma_start(T.wb[:], T.w[:]).then_inc(T.sem.ldw, 16)
        for h, (c0, c1) in enumerate(pieces[rank]):
            g.vector.wait_ge(T.sem["ldx%d" % h], 16)
            g.vector.quantize_mx(T.xq[:, a + c0:a + c1], T.xs[:, a + c0:a + c1],
                                 T.xb[:, 4 * c0:4 * c1]).then_inc(T.sem["qx%d" % h], 1)
        g.vector.wait_ge(T.sem.ldw, 16)
        g.vector.quantize_mx(T.wq[:], T.ws[:], T.wb[:]).then_inc(T.sem.qw, 1)

    seen = {}

    def wait(q, tag, sem, val):
        if seen.get((tag, sem), 0) < val:
            q.wait_ge(T.sem[sem], val)
            seen[(tag, sem)] = val

    for _, j, kind, xfers, lsem in mine:
        part, h0, h1 = kind
        if cores[j] == core:
            for h in range(h0, h1 + 1):
                wait(g, "g", "qx%d" % h, 1)
        else:
            wait(g, "g", *arr[(core, j, kind)])
        sem = T.sem["a%s%d%d" % (part, slot[j], h0)]
        trs = []
        for dsts, eng, u, v in xfers:
            ap, ids = view(j, part, u, v), []
            for d in dsts:
                rid, pid, _ = topo.addr(d)
                ids.append(DstId(rid=rid, pnc=pid))
            trs.append(RemoteDMATransfer(dst_ids=ids, dma_engine_mask=sum(1 << b for b in eng), remote_sem=sem,
                                         srcs=[ap], dsts=[ap for _ in dsts]))
        g.remote_dma_fused(trs, local_sem=T.sem[lsem])
    for lsem in sorted(totals):
        g.wait_ge(T.sem[lsem], totals[lsem])
    if rank is None:
        return

    tiles = sorted((0.0 if j == rank else key[(core, j)], WID[j], j)
                   for j in range(len(cores)) if SEQ[j] == SEQ[rank])
    g.tensor.wait_ge(T.sem.qw, 1)
    g.sync.wait_ge(T.sem.sc, totals["sc"])
    b = 0
    for _, _, j in tiles:
        hs = list(range(len(pieces[j])))
        if j != rank:
            hs.reverse()
        for h in hs:
            if j == rank:
                wait(g.tensor, "t", "qx%d" % h, 1)
            else:
                for sem in sorted(need[(core, j, h)]):
                    wait(g.tensor, "t", sem, need[(core, j, h)][sem])
            c0, c1 = pieces[j][h]
            a, y0, y1 = SLOT * slot[j], yoff[j] + c0, yoff[j] + c1
            g.tensor.matmul_mx(T.ps[:, 512 * b:512 * b + c1 - c0], T.wq[:], T.ws[:], T.xq[:, a + c0:a + c1],
                               T.xs[:, a + c0:a + c1], True, True).then_inc(T.sem["mm%d" % b], 1)
            if b % 2 == 0:
                g.vector.wait_ge(T.sem["mm%d" % b], 1)
                g.vector.tensor_copy(T.ysb[:, y0:y1],
                                     T.ps[:, 512 * b:512 * b + c1 - c0]).then_inc(T.sem["cp%d" % b], 1)
            else:
                g.scalar.wait_ge(T.sem["mm%d" % b], 1)
                g.scalar.activation(T.ysb[:, y0:y1], T.ps[:, 512 * b:512 * b + c1 - c0],
                                    ActivationFunctionType.Copy).then_inc(T.sem["cp%d" % b], 1)
            g.sync.wait_ge(T.sem["cp%d" % b], 1)
            b += 1
        g.sync.dma_start(T.y[:, yoff[j]:yoff[j] + WID[j]],
                         T.ysb[:, yoff[j]:yoff[j] + WID[j]]).then_inc(T.sem.st, 16)
    g.sync.wait_ge(T.sem.st, 16 * len(tiles))
